import numpy as np
import ml_dtypes


def mxq(x, axis, fmt="e4m3"):
    dtype, down = {"e4m3": (ml_dtypes.float8_e4m3fn, 7), "e5m2": (ml_dtypes.float8_e5m2, 14)}[fmt]
    v = np.moveaxis(np.asarray(x, np.float32).astype(ml_dtypes.bfloat16).astype(np.float64), axis, -1)
    blocks = v.reshape(v.shape[:-1] + (-1, 32))
    amax = np.abs(blocks).max(-1, keepdims=True)
    byte = np.maximum(np.where(amax > 0, np.frexp(amax)[1] - 1 + 127, 0) - down, 1)
    scale = np.exp2(byte - 127.0)
    codes = (blocks / scale).astype(np.float32).astype(dtype).astype(np.float64)
    return np.moveaxis((codes * scale).reshape(v.shape), -1, axis)


WIDE = False


def mx_kscale(k):
    if not WIDE:
        return np.ones(k)
    levels = np.array([10, -10, 5, -5, 0])
    if k % 512:
        return np.exp2(np.random.permutation(np.resize(levels, k // 32))).repeat(32)
    a = np.empty((k // 512, 16))
    for p in range(k // 512):
        a[p, :8] = np.random.permutation(np.resize(levels, 8))
        for g in range(8):
            far = levels[np.abs(levels - a[p, g]) >= 10]
            a[p, g + 8] = far[np.random.randint(len(far))]
    return np.exp2(a.ravel()).repeat(32)


def f64(x):
    return np.asarray(x).astype(np.float64)


def striped(idx):
    return np.tile(idx.reshape(-1, 16).T, (8, 1)).astype(np.uint16)


def unstriped(offs):
    return offs[:16].T.reshape(-1).astype(np.int64)


def striped8(idx):
    return np.concatenate([x.reshape(-1, 16).T for x in idx]).astype(np.uint16)


def runs(offs, k):
    lists = np.stack([offs[16 * r : 16 * r + 16].T.reshape(-1) for r in range(8)]).astype(np.int64)
    return lists[np.arange(k) % 512 // 64]


def pack_weight(w):
    k, n = w.shape
    w = f64(np.asarray(w, np.float32).astype(ml_dtypes.bfloat16)).reshape(k // 32, 32, n)
    amax = np.abs(w).max(1)
    byte = np.clip(np.where(amax > 0, np.frexp(amax)[1] - 1 + 127 - 7, 1), 1, 254)
    scaled = (w * np.exp2(127.0 - byte)[:, None, :]).reshape(k, n).astype(np.float32)
    words = np.ascontiguousarray(scaled.reshape(k // 512, 128, 4, n).transpose(0, 1, 3, 2)).astype(ml_dtypes.float8_e4m3fn).view(np.uint8)
    return words, np.ascontiguousarray(byte.astype(np.uint8).reshape(k // 512, 16, n))


def unpack_weight(words, scales):
    g, p, n, _ = words.shape
    vals = np.ascontiguousarray(words).view(ml_dtypes.float8_e4m3fn).astype(np.float64) * np.repeat(np.exp2(scales.astype(np.float64) - 127.0), 8, axis=1)[..., None]
    return vals.transpose(0, 1, 3, 2).reshape(g * 512, n)


E2M1 = np.array([0.0, 0.5, 1.0, 1.5, 2.0, 3.0, 4.0, 6.0, -0.0, -0.5, -1.0, -1.5, -2.0, -3.0, -4.0, -6.0])


def pack_fp4(w):
    k, n = w.shape
    w = f64(np.asarray(w, np.float32).astype(ml_dtypes.bfloat16)).reshape(k // 32, 32, n)
    amax = np.abs(w).max(1)
    mant, ex = np.frexp(amax / 6.0)
    byte = np.clip(np.where(amax > 0, np.where(mant > 0.5, ex, ex - 1) + 127, 1), 1, 254)
    scaled = (w * np.exp2(127.0 - byte)[:, None, :]).reshape(k, n).astype(np.float32)
    c = np.ascontiguousarray(scaled.reshape(k // 512, 128, 4, n).transpose(0, 1, 3, 2)).astype(ml_dtypes.float4_e2m1fn).view(np.uint8) & 0xF
    words = (c[..., 0::2] | (c[..., 1::2] << 4)).reshape(k // 512, 128, 2 * n)
    return np.ascontiguousarray(words), np.ascontiguousarray(byte.astype(np.uint8).reshape(k // 512, 16, n))


def unpack_fp4(words, scales):
    g, _, n = scales.shape
    words = np.ascontiguousarray(words).reshape(g, 128, n, 2)
    nib = np.empty((g, 128, n, 4), np.uint8)
    nib[..., 0::2] = words & 0xF
    nib[..., 1::2] = words >> 4
    vals = E2M1[nib] * np.repeat(np.exp2(scales.astype(np.float64) - 127.0), 8, axis=1)[..., None]
    return vals.transpose(0, 1, 3, 2).reshape(g * 512, n)


def sigmoid(v):
    return 1.0 / (1.0 + np.exp(-np.maximum(v, -700.0)))

def planes(y):
    n, m = y.shape
    v = y.astype(np.float32).astype(ml_dtypes.bfloat16).astype(np.float64).reshape(n // 32, 32, m)
    top = np.abs(v).max(1)
    byte = np.clip(np.where(top > 0, np.frexp(top)[1] - 1 + 127 - 7, 1), 1, 254)
    codes = (v * np.exp2(127.0 - byte)[:, None, :]).reshape(n, m).astype(np.float32).astype(ml_dtypes.float8_e4m3fn).view(np.uint8)
    words = codes.reshape(n // 512, 128, 4, m).transpose(0, 1, 3, 2)
    return np.ascontiguousarray(words), np.ascontiguousarray(byte.astype(np.uint8).reshape(n // 512, 16, m))


K, T, S, H, C = 512, 2048, 512, 512, 512


def setup_inputs():
    n = np.random.standard_normal
    s = mx_kscale(K)[:, None]
    packed_xT = pack_weight(n((K, T)) * s)
    packed_w1 = pack_fp4(n((K, H)) / np.sqrt(K) / s)
    return {
        "x_words": packed_xT[0],
        "x_scales": packed_xT[1],
        "w1_words": packed_w1[0],
        "w1_scales": packed_w1[1],
        "tau": np.random.uniform(0.3, 0.9, (H, 1)).astype(np.float32),
        "gs": (np.random.uniform(0.5, 1.5, (K, 1)) / s).astype(np.float32),
        "sl": np.random.uniform(1.5, 3.0, (C, 1)).astype(np.float32),
        "th": (0.5 * n((C, 1))).astype(np.float32),
        "offs": striped(np.random.permutation(T)[:S]),
        "n1": striped(np.random.permutation(S)),
        "n2": striped(np.random.permutation(S)),
        "cand": striped(np.random.permutation(T)[:C]),
        "n3": striped8(np.stack([np.random.permutation(S) for _ in range(8)])),
        "n4": striped8(np.stack([np.random.permutation(S) for _ in range(8)])),
    }


def reference(x_words, x_scales, w1_words, w1_scales, tau, gs, sl, th, offs, n1, n2, cand, n3, n4):
    x_cand = unpack_weight(x_words, x_scales)[:, unstriped(cand)]
    xq = unpack_weight(x_words, x_scales)[:, unstriped(offs)]
    y = unpack_fp4(w1_words, w1_scales).T @ xq
    top = y.max(axis=1, keepdims=True)
    ea = np.exp(f64(tau) * (y[:, unstriped(n1)] - top))
    sm = y * ea
    ds = np.zeros((H, S))
    ds[:, unstriped(n2)] = sm
    z = f64(gs) * (2.0 * ds - (0.5 * y))
    s = 0.0625 * ((x_cand.T @ mxq(z, 0, "e4m3")))
    sg = sigmoid(f64(sl) * (s[np.arange(C)[:, None], runs(n3, C)] - f64(th)))
    out_0 = 1.5 * (s * (sg - (sg[np.arange(C)[:, None], runs(n4, C)])))
    return (out_0,) + planes(out_0)

@@ -1,0 +1,218 @@
+from contextlib import ExitStack
+
+import concourse.mybir as mybir
+
+K, T, S, H, C = 512, 2048, 512, 512, 512
+FLOPS = 2 * K * H * S + 2 * K * C * S
+
+F32 = mybir.dt.float32
+BF16 = mybir.dt.bfloat16
+I32 = mybir.dt.int32
+U32 = mybir.dt.uint32
+U16 = mybir.dt.uint16
+U8 = mybir.dt.uint8
+FP8X4 = mybir.dt.float8_e4m3fn_x4
+FP4X4 = mybir.dt.float4_e2m1fn_x4
+ALU = mybir.AluOpType
+ACT = mybir.ActivationFunctionType
+
+P = 128
+PACK = 4
+LANE = 16
+HALF = S // 2
+WIDE = 704
+
+
+def tile_picked_candesdedb_none_po_kernel(
+    tc, x_words, x_scales, w1_words, w1_scales, tau, gs, sl, th, offs, n1, n2, cand, n3, n4, out_0, out_1, out_2
+):
+    nc = tc.nc
+    with ExitStack() as ctx:
+        pool = ctx.enter_context(tc.tile_pool(name="keep", bufs=1))
+        psum = ctx.enter_context(tc.psum_pool(name="psum", bufs=1))
+
+        def sb(name, shape, dtype, after=None):
+            return pool.tile(shape, dtype, name=name, tag=after or name, align_bytes=64)
+
+        def load_list(name, src):
+            tile = sb(name, [P, S // LANE], U16)
+            nc.sync.dma_start(tile[:], src)
+            return tile
+
+        def load_rows(name, src):
+            tile = sb(name, [P, PACK], F32)
+            nc.sync.dma_start(tile[:], src.rearrange("(p t) o -> p (t o)", t=PACK))
+            return tile
+
+        def entries(lst, lo, hi):
+            return lst[:, lo // LANE : hi // LANE]
+
+        xs = sb("xs", [P, T], U8)
+        ws_raw = sb("ws_raw", [P, H], U8)
+        nc.vector.memset(xs[:].bitcast(I32), 0)
+        nc.gpsimd.memset(ws_raw[:].bitcast(I32), 0)
+
+        offs_t = load_list("offs_t", offs)
+        ww_raw = sb("ww_raw", [P, 2 * H], U8)
+        nc.scalar.dma_start(ww_raw[:].bitcast(I32), w1_words[0].bitcast(I32))
+        cand_t = load_list("cand_t", cand)
+        for q in range(4):
+            queue = nc.sync if q < 2 else nc.scalar
+            queue.dma_start(xs[32 * q : 32 * q + 4, :].bitcast(I32), x_scales[0, 4 * q : 4 * q + 4, :].bitcast(I32))
+        xw = sb("xw", [P, T], I32)
+        nc.sync.dma_start(xw[:], x_words[0].rearrange("p n r -> p (n r)").bitcast(I32))
+        for q in range(4):
+            nc.sync.dma_start(
+                ws_raw[32 * q : 32 * q + 4, :].bitcast(I32), w1_scales[0, 4 * q : 4 * q + 4, :].bitcast(I32)
+            )
+        n1_t = load_list("n1_t", n1)
+        tau_t = load_rows("tau_t", tau)
+        gs_t = load_rows("gs_t", gs)
+        sl_t = load_rows("sl_t", sl)
+        th_t = load_rows("th_t", th)
+        n2_t = load_list("n2_t", n2)
+        n3_t = load_list("n3_t", n3)
+        n4_t = load_list("n4_t", n4)
+
+        ww = sb("ww", [P, 2 * H], U8)
+        nc.scalar.copy(
+            ww[:].bitcast(U16).rearrange("p (t m) -> p t m", t=PACK),
+            ww_raw[:].bitcast(U16).rearrange("p (m t) -> p t m", t=PACK),
+        )
+
+        xq_s = sb("xq_s", [P, S], U8)
+        xq_w = sb("xq_w", [P, S], U32)
+        nc.vector.tensor_copy(xq_s[:], xs[:].indirect(offs_t[:]))
+        ws = sb("ws", [P, H], U8)
+        nc.gpsimd.tensor_copy(
+            ws[:].rearrange("p (t m) -> p t m", t=PACK), ws_raw[:].rearrange("p (m t) -> p t m", t=PACK)
+        )
+        nc.vector.tensor_copy(xq_w[:], xw[:].bitcast(U32).indirect(offs_t[:]))
+
+        xc_s = sb("xc_s", [P, C], U8)
+        nc.vector.tensor_copy(xc_s[:].rearrange("p (t m) -> p m t", t=PACK), xs[:].indirect(cand_t[:]))
+
+        gs2 = sb("gs2", [P, PACK], F32)
+        ngs = sb("ngs", [P, PACK], F32)
+        nc.gpsimd.tensor_scalar(gs2[:], gs_t[:], 2.0, 0.0, ALU.mult, ALU.add)
+        nc.gpsimd.tensor_scalar(ngs[:], gs_t[:], -0.5, 0.0, ALU.mult, ALU.add)
+        nsl = sb("nsl", [P, PACK], F32)
+        sbias = sb("sbias", [P, PACK], F32)
+        nc.scalar.mul(nsl[:], sl_t[:], -1.0)
+        nc.gpsimd.tensor_tensor(sbias[:], nsl[:], th_t[:], ALU.mult)
+
+        y_ps = [psum.tile([P, S], F32, name="y_ps%d" % t) for t in range(PACK)]
+        s_ps = [psum.tile([P, S], F32, name="s_ps%d" % t) for t in range(PACK)]
+        for t in range(PACK):
+            nc.tensor.matmul_mx(
+                out=y_ps[t][:],
+                lhsT=ww[:, 2 * P * t : 2 * P * (t + 1)].bitcast(FP4X4),
+                lhsT_scale=ws[:, P * t : P * (t + 1)],
+                rhs=xq_w[:].bitcast(FP8X4),
+                rhs_scale=xq_s[:],
+                start=True,
+                stop=True,
+            )
+
+
+        y = [sb("y%d" % t, [P, 2 * S], F32) for t in range(PACK)]
+        top = [sb("top%d" % t, [P, 1], F32) for t in range(PACK)]
+        ebias = [sb("ebias%d" % t, [P, 1], F32) for t in range(PACK)]
+        ea = [sb("ea%d" % t, [P, S], F32) for t in range(PACK)]
+        pre = [sb("pre%d" % t, [P, S], F32) for t in range(PACK)]
+        for t in range(PACK):
+            nc.vector.tensor_scalar(y[t][:, :S], y_ps[t][:], 1.0, None, ALU.mult, ALU.max, accum_out=top[t][:])
+            nc.gpsimd.tensor_scalar(ebias[t][:], top[t][:], tau_t[:, t : t + 1], -1.0, ALU.mult, ALU.mult)
+            if t in (0, 3):
+                nc.gpsimd.tensor_scalar(pre[t][:], y[t][:, :S], gs2[:, t : t + 1], 0.0, ALU.mult, ALU.add)
+            nc.scalar.activation(
+                ea[t][:], y[t][:].indirect(n1_t[:]), ACT.Exp, bias=ebias[t][:], scale=tau_t[:, t : t + 1]
+            )
+
+
+        xc_w = sb("xc_w", [P, C], U32, "xq_w")
+        nc.vector.tensor_copy(xc_w[:].rearrange("p (t m) -> p m t", t=PACK), xw[:].bitcast(U32).indirect(cand_t[:]))
+        for t in (1, 2):
+            nc.vector.scalar_tensor_tensor(pre[t][:], y_ps[t][:], gs2[:, t : t + 1], ea[t][:], ALU.mult, ALU.mult)
+        ds2 = [sb("ds2_%d" % t, [P, WIDE if t in (0, 3) else S], F32, "ea2" if t == 0 else None) for t in range(PACK)]
+        z = sb("z", [P, PACK, S], BF16)
+        for lo in (0, HALF):
+            for t in (1, 2):
+                nc.scalar.activation(
+                    ds2[t][:].indirect(entries(n2_t, lo, lo + HALF)), pre[t][:, lo : lo + HALF], ACT.Copy
+                )
+        for t in (0, 3):
+            nc.vector.tensor_tensor(ds2[t][:].indirect(n2_t[:]), pre[t][:], ea[t][:], ALU.mult)
+        for t in (0, 1, 3, 2):
+            nc.vector.scalar_tensor_tensor(
+                z[:, t, :], y_ps[t][:], ngs[:, t : t + 1], ds2[t][:, :S], ALU.mult, ALU.add
+            )
+
+        def weave(engine_copy, dst, src, lo, hi):
+            engine_copy(
+                dst[:, lo:hi, :].rearrange("p (c i) t -> p c t i", i=4),
+                src[:, :, lo:hi].rearrange("p t (c i) -> p c t i", i=4),
+            )
+
+        cut = 192
+        zw = sb("zw", [P, S, PACK], BF16)
+        weave(nc.scalar.copy, zw, z, 0, cut)
+        weave(nc.vector.tensor_copy, zw, z, cut, S)
+        zq = sb("zq", [P, S], U32)
+        zs = sb("zs", [P, S], U8)
+        nc.vector.quantize_mx(out=zq[:].bitcast(FP8X4), scales=zs[:], in_=zw[:].rearrange("p c t -> p (c t)"))
+
+        for t in range(PACK):
+            nc.tensor.matmul_mx(
+                out=s_ps[t][:],
+                lhsT=xc_w[:, P * t : P * (t + 1)].bitcast(FP8X4),
+                lhsT_scale=xc_s[:, P * t : P * (t + 1)],
+                rhs=zq[:].bitcast(FP8X4),
+                rhs_scale=zs[:],
+                start=True,
+                stop=True,
+            )
+
+        s = [sb("s%d" % t, [P, 2 * S], F32) for t in range(PACK)]
+        sg = [sb("sg%d" % t, [P, 2 * S], F32) for t in range(PACK)]
+        diff = [sb("diff%d" % t, [P, S], F32) for t in range(PACK)]
+        res = sb("res", [P, PACK, S], F32)
+        for t in range(PACK):
+            nc.vector.tensor_scalar(s[t][:, :S], s_ps[t][:], 0.0625, None, ALU.mult)
+            nc.scalar.activation(
+                sg[t][:, :S],
+                s[t][:].indirect(n3_t[:]),
+                ACT.Sigmoid,
+                bias=sbias[:, t : t + 1],
+                scale=sl_t[:, t : t + 1],
+            )
+        other = [sb("other%d" % t, [P, S], F32, "s3" if t == 2 else None) for t in range(PACK)]
+        out_rows = out_0.rearrange("(p t) c -> p t c", t=PACK)
+
+        def finish(t, cols):
+            nc.vector.scalar_tensor_tensor(
+                res[:, t, cols], diff[t][:, cols], -1.5 * 0.0625, s_ps[t][:, cols], ALU.mult, ALU.mult
+            )
+
+        for t in (0, 1):
+            nc.vector.tensor_copy(other[t][:], sg[t][:, :S])
+            nc.vector.tensor_tensor(diff[t][:], sg[t][:].indirect(n4_t[:]), other[t][:], ALU.subtract)
+            finish(t, slice(0, S))
+            nc.sync.dma_start(out_rows[:, t, :], res[:, t, :])
+        for t, pieces in ((2, ((0, S),)), (3, ((0, HALF), (HALF, S)))):
+            for lo, hi in pieces:
+                nc.scalar.activation(other[t][:, lo:hi], sg[t][:].indirect(entries(n4_t, lo, hi)), ACT.Copy)
+                nc.vector.tensor_tensor(diff[t][:, lo:hi], other[t][:, lo:hi], sg[t][:, lo:hi], ALU.subtract)
+                finish(t, slice(lo, hi))
+            nc.sync.dma_start(out_rows[:, t, :], res[:, t, :])
+
+        rw = sb("rw", [P, S, PACK], BF16)
+        weave(nc.scalar.copy, rw, res, 0, cut)
+        weave(nc.vector.tensor_copy, rw, res, cut, S)
+        rq = sb("rq", [P, S], U32)
+        rs = sb("rs", [P, S], U8)
+        nc.vector.quantize_mx(out=rq[:].bitcast(FP8X4), scales=rs[:], in_=rw[:].rearrange("p c t -> p (c t)"))
+        nc.sync.dma_start(out_1[0].rearrange("p c r -> p (c r)").bitcast(I32), rq[:].bitcast(I32))
+        for q in range(4):
+            queue = nc.scalar if q % 2 else nc.sync
+            queue.dma_start(out_2[0, 4 * q : 4 * q + 4, :].bitcast(I32), rs[32 * q : 32 * q + 4, :].bitcast(I32))

@@ -50,7 +50,7 @@ def tile_picked_candesdedb_none_po_kernel(
         xs = sb("xs", [P, T], U8)
         ws_raw = sb("ws_raw", [P, H], U8)
         nc.vector.memset(xs[:].bitcast(I32), 0)
-        nc.gpsimd.memset(ws_raw[:].bitcast(I32), 0)
+        nc.vector.memset(ws_raw[:].bitcast(I32), 0)
 
         offs_t = load_list("offs_t", offs)
         ww_raw = sb("ww_raw", [P, 2 * H], U8)
@@ -84,7 +84,7 @@ def tile_picked_candesdedb_none_po_kernel(
         xq_w = sb("xq_w", [P, S], U32)
         nc.vector.tensor_copy(xq_s[:], xs[:].indirect(offs_t[:]))
         ws = sb("ws", [P, H], U8)
-        nc.gpsimd.tensor_copy(
+        nc.vector.tensor_copy(
             ws[:].rearrange("p (t m) -> p t m", t=PACK), ws_raw[:].rearrange("p (m t) -> p t m", t=PACK)
         )
         nc.vector.tensor_copy(xq_w[:], xw[:].bitcast(U32).indirect(offs_t[:]))
@@ -92,14 +92,16 @@ def tile_picked_candesdedb_none_po_kernel(
         xc_s = sb("xc_s", [P, C], U8)
         nc.vector.tensor_copy(xc_s[:].rearrange("p (t m) -> p m t", t=PACK), xs[:].indirect(cand_t[:]))
 
+        xc_w = sb("xc_w", [P, C], U32, "ws_raw")
+        nc.vector.tensor_copy(xc_w[:].rearrange("p (t m) -> p m t", t=PACK), xw[:].bitcast(U32).indirect(cand_t[:]))
+
         gs2 = sb("gs2", [P, PACK], F32)
         ngs = sb("ngs", [P, PACK], F32)
-        nc.gpsimd.tensor_scalar(gs2[:], gs_t[:], 2.0, 0.0, ALU.mult, ALU.add)
-        nc.gpsimd.tensor_scalar(ngs[:], gs_t[:], -0.5, 0.0, ALU.mult, ALU.add)
+        nc.scalar.mul(gs2[:], gs_t[:], 2.0)
+        nc.scalar.mul(ngs[:], gs_t[:], -0.5)
         nsl = sb("nsl", [P, PACK], F32)
         sbias = sb("sbias", [P, PACK], F32)
         nc.scalar.mul(nsl[:], sl_t[:], -1.0)
-        nc.gpsimd.tensor_tensor(sbias[:], nsl[:], th_t[:], ALU.mult)
 
         y_ps = [psum.tile([P, S], F32, name="y_ps%d" % t) for t in range(PACK)]
         s_ps = [psum.tile([P, S], F32, name="s_ps%d" % t) for t in range(PACK)]
@@ -123,62 +125,90 @@ def tile_picked_candesdedb_none_po_kernel(
         for t in range(PACK):
             nc.vector.tensor_scalar(y[t][:, :S], y_ps[t][:], 1.0, None, ALU.mult, ALU.max, accum_out=top[t][:])
             nc.gpsimd.tensor_scalar(ebias[t][:], top[t][:], tau_t[:, t : t + 1], -1.0, ALU.mult, ALU.mult)
-            if t in (0, 3):
+            if t == 0:
                 nc.gpsimd.tensor_scalar(pre[t][:], y[t][:, :S], gs2[:, t : t + 1], 0.0, ALU.mult, ALU.add)
             nc.scalar.activation(
                 ea[t][:], y[t][:].indirect(n1_t[:]), ACT.Exp, bias=ebias[t][:], scale=tau_t[:, t : t + 1]
             )
 
 
-        xc_w = sb("xc_w", [P, C], U32, "xq_w")
-        nc.vector.tensor_copy(xc_w[:].rearrange("p (t m) -> p m t", t=PACK), xw[:].bitcast(U32).indirect(cand_t[:]))
-        for t in (1, 2):
-            nc.vector.scalar_tensor_tensor(pre[t][:], y_ps[t][:], gs2[:, t : t + 1], ea[t][:], ALU.mult, ALU.mult)
-        ds2 = [sb("ds2_%d" % t, [P, WIDE if t in (0, 3) else S], F32, "ea2" if t == 0 else None) for t in range(PACK)]
+        nc.vector.tensor_scalar(pre[3][:], y[3][:, :S], gs2[:, 3:4], None, ALU.mult)
+        nc.vector.tensor_tensor(sbias[:], nsl[:], th_t[:], ALU.mult)
         z = sb("z", [P, PACK, S], BF16)
+
+        def product(t):
+            nc.vector.scalar_tensor_tensor(pre[t][:], y_ps[t][:], gs2[:, t : t + 1], ea[t][:], ALU.mult, ALU.mult)
+
+        product(1)
+        ds2 = [sb("ds2_%d" % t, [P, WIDE if t == 3 else S], F32, "ea1" if t == 0 else None) for t in range(PACK)]
+
+        def scatter_half_on_vector(t, lo):
+            cols = slice(lo, lo + HALF)
+            nc.vector.tensor_tensor(
+                ds2[t][:].indirect(entries(n2_t, lo, lo + HALF)), pre[t][:, cols], ea[t][:, cols], ALU.mult
+            )
+
+        scatter_half_on_vector(0, 0)
+        product(2)
+        scatter_half_on_vector(0, HALF)
         for lo in (0, HALF):
             for t in (1, 2):
                 nc.scalar.activation(
                     ds2[t][:].indirect(entries(n2_t, lo, lo + HALF)), pre[t][:, lo : lo + HALF], ACT.Copy
                 )
-        for t in (0, 3):
-            nc.vector.tensor_tensor(ds2[t][:].indirect(n2_t[:]), pre[t][:], ea[t][:], ALU.mult)
-        for t in (0, 1, 3, 2):
+        nc.vector.tensor_tensor(ds2[3][:].indirect(n2_t[:]), pre[3][:], ea[3][:], ALU.mult)
+        halves = (slice(0, HALF), slice(HALF, S))
+
+        def make_z(t, cols):
             nc.vector.scalar_tensor_tensor(
-                z[:, t, :], y_ps[t][:], ngs[:, t : t + 1], ds2[t][:, :S], ALU.mult, ALU.add
+                z[:, t, cols], y_ps[t][:, cols], ngs[:, t : t + 1], ds2[t][:, cols], ALU.mult, ALU.add
             )
 
-        def weave(engine_copy, dst, src, lo, hi):
-            engine_copy(
-                dst[:, lo:hi, :].rearrange("p (c i) t -> p c t i", i=4),
-                src[:, :, lo:hi].rearrange("p t (c i) -> p c t i", i=4),
-            )
+        for t in (0, 1, 3):
+            make_z(t, slice(0, S))
+        for cols in halves:
+            make_z(2, cols)
 
-        cut = 192
-        zw = sb("zw", [P, S, PACK], BF16)
-        weave(nc.scalar.copy, zw, z, 0, cut)
-        weave(nc.vector.tensor_copy, zw, z, cut, S)
-        zq = sb("zq", [P, S], U32)
-        zs = sb("zs", [P, S], U8)
-        nc.vector.quantize_mx(out=zq[:].bitcast(FP8X4), scales=zs[:], in_=zw[:].rearrange("p c t -> p (c t)"))
+        def quantise(name, src):
+            woven = sb(name + "_woven", [P, S, PACK], BF16)
+            codes = sb(name + "_codes", [P, S], U32)
+            scales = sb(name + "_scales", [P, S], U8)
+            for cols, copy in zip(halves, (nc.scalar.copy, nc.vector.tensor_copy)):
+                copy(
+                    woven[:, cols, :].rearrange("p (c i) t -> p c t i", i=4),
+                    src[:, :, cols].rearrange("p t (c i) -> p c t i", i=4),
+                )
+            for cols in reversed(halves):
+                nc.vector.quantize_mx(
+                    out=codes[:, cols].bitcast(FP8X4),
+                    scales=scales[:, cols],
+                    in_=woven[:, cols, :].rearrange("p c t -> p (c t)"),
+                )
+            return codes, scales
+
+        zq, zs = quantise("z", z)
 
         for t in range(PACK):
-            nc.tensor.matmul_mx(
-                out=s_ps[t][:],
-                lhsT=xc_w[:, P * t : P * (t + 1)].bitcast(FP8X4),
-                lhsT_scale=xc_s[:, P * t : P * (t + 1)],
-                rhs=zq[:].bitcast(FP8X4),
-                rhs_scale=zs[:],
-                start=True,
-                stop=True,
-            )
+            for cols in reversed(halves):
+                nc.tensor.matmul_mx(
+                    out=s_ps[t][:, cols],
+                    lhsT=xc_w[:, P * t : P * (t + 1)].bitcast(FP8X4),
+                    lhsT_scale=xc_s[:, P * t : P * (t + 1)],
+                    rhs=zq[:, cols].bitcast(FP8X4),
+                    rhs_scale=zs[:, cols],
+                    start=True,
+                    stop=True,
+                )
 
         s = [sb("s%d" % t, [P, 2 * S], F32) for t in range(PACK)]
         sg = [sb("sg%d" % t, [P, 2 * S], F32) for t in range(PACK)]
         diff = [sb("diff%d" % t, [P, S], F32) for t in range(PACK)]
         res = sb("res", [P, PACK, S], F32)
         for t in range(PACK):
-            nc.vector.tensor_scalar(s[t][:, :S], s_ps[t][:], 0.0625, None, ALU.mult)
+            if t < 3:
+                nc.vector.tensor_scalar(s[t][:, :S], s_ps[t][:], 0.0625, None, ALU.mult)
+            else:
+                nc.scalar.mul(s[t][:, :S], s_ps[t][:], 0.0625)
             nc.scalar.activation(
                 sg[t][:, :S],
                 s[t][:].indirect(n3_t[:]),
@@ -206,13 +236,10 @@ def tile_picked_candesdedb_none_po_kernel(
                 finish(t, slice(lo, hi))
             nc.sync.dma_start(out_rows[:, t, :], res[:, t, :])
 
-        rw = sb("rw", [P, S, PACK], BF16)
-        weave(nc.scalar.copy, rw, res, 0, cut)
-        weave(nc.vector.tensor_copy, rw, res, cut, S)
-        rq = sb("rq", [P, S], U32)
-        rs = sb("rs", [P, S], U8)
-        nc.vector.quantize_mx(out=rq[:].bitcast(FP8X4), scales=rs[:], in_=rw[:].rearrange("p c t -> p (c t)"))
-        nc.sync.dma_start(out_1[0].rearrange("p c r -> p (c r)").bitcast(I32), rq[:].bitcast(I32))
+        rq, rs = quantise("res", res)
+        out_words = out_1[0].rearrange("p c r -> p (c r)").bitcast(I32)
+        for cols in reversed(halves):
+            nc.sync.dma_start(out_words[:, cols], rq[:, cols].bitcast(I32))
         for q in range(4):
             queue = nc.scalar if q % 2 else nc.sync
             queue.dma_start(out_2[0, 4 * q : 4 * q + 4, :].bitcast(I32), rs[32 * q : 32 * q + 4, :].bitcast(I32))

@@ -84,13 +84,13 @@ def tile_picked_candesdedb_none_po_kernel(
         xq_w = sb("xq_w", [P, S], U32)
         nc.vector.tensor_copy(xq_s[:], xs[:].indirect(offs_t[:]))
         ws = sb("ws", [P, H], U8)
-        nc.vector.tensor_copy(
+        nc.gpsimd.tensor_copy(
             ws[:].rearrange("p (t m) -> p t m", t=PACK), ws_raw[:].rearrange("p (m t) -> p t m", t=PACK)
         )
         nc.vector.tensor_copy(xq_w[:], xw[:].bitcast(U32).indirect(offs_t[:]))
 
-        xc_s = sb("xc_s", [P, C], U8)
-        nc.vector.tensor_copy(xc_s[:].rearrange("p (t m) -> p m t", t=PACK), xs[:].indirect(cand_t[:]))
+        xc_s_raw = sb("xc_s_raw", [P, C], U8)
+        nc.vector.tensor_copy(xc_s_raw[:], xs[:].indirect(cand_t[:]))
 
         xc_w = sb("xc_w", [P, C], U32, "ws_raw")
         nc.vector.tensor_copy(xc_w[:].rearrange("p (t m) -> p m t", t=PACK), xw[:].bitcast(U32).indirect(cand_t[:]))
@@ -133,6 +133,10 @@ def tile_picked_candesdedb_none_po_kernel(
 
 
         nc.vector.tensor_scalar(pre[3][:], y[3][:, :S], gs2[:, 3:4], None, ALU.mult)
+        xc_s = sb("xc_s", [P, C], U8, "xq_s")
+        nc.vector.tensor_copy(
+            xc_s[:].rearrange("p (t m) -> p t m", t=PACK), xc_s_raw[:].rearrange("p (m t) -> p t m", t=PACK)
+        )
         nc.vector.tensor_tensor(sbias[:], nsl[:], th_t[:], ALU.mult)
         z = sb("z", [P, PACK, S], BF16)
 
@@ -169,16 +173,19 @@ def tile_picked_candesdedb_none_po_kernel(
         for cols in halves:
             make_z(2, cols)
 
-        def quantise(name, src):
+        def quantise(name, src, scalar_columns, order):
             woven = sb(name + "_woven", [P, S, PACK], BF16)
             codes = sb(name + "_codes", [P, S], U32)
             scales = sb(name + "_scales", [P, S], U8)
-            for cols, copy in zip(halves, (nc.scalar.copy, nc.vector.tensor_copy)):
+            pieces = [(nc.scalar.copy, halves[0]), (nc.vector.tensor_copy, slice(scalar_columns, S))]
+            if scalar_columns > HALF:
+                pieces.append((nc.scalar.copy, slice(HALF, scalar_columns)))
+            for copy, cols in pieces:
                 copy(
                     woven[:, cols, :].rearrange("p (c i) t -> p c t i", i=4),
                     src[:, :, cols].rearrange("p t (c i) -> p c t i", i=4),
                 )
-            for cols in reversed(halves):
+            for cols in order:
                 nc.vector.quantize_mx(
                     out=codes[:, cols].bitcast(FP8X4),
                     scales=scales[:, cols],
@@ -186,7 +193,7 @@ def tile_picked_candesdedb_none_po_kernel(
                 )
             return codes, scales
 
-        zq, zs = quantise("z", z)
+        zq, zs = quantise("z", z, HALF, halves[::-1])
 
         for t in range(PACK):
             for cols in reversed(halves):
@@ -200,7 +207,7 @@ def tile_picked_candesdedb_none_po_kernel(
                     stop=True,
                 )
 
-        s = [sb("s%d" % t, [P, 2 * S], F32) for t in range(PACK)]
+        s = [sb("s%d" % t, [P, 2 * S], F32) for t in range(PACK - 1)]
         sg = [sb("sg%d" % t, [P, 2 * S], F32) for t in range(PACK)]
         diff = [sb("diff%d" % t, [P, S], F32) for t in range(PACK)]
         res = sb("res", [P, PACK, S], F32)
@@ -208,6 +215,7 @@ def tile_picked_candesdedb_none_po_kernel(
             if t < 3:
                 nc.vector.tensor_scalar(s[t][:, :S], s_ps[t][:], 0.0625, None, ALU.mult)
             else:
+                s.append(sb("s3", [P, 2 * S], F32, "s0"))
                 nc.scalar.mul(s[t][:, :S], s_ps[t][:], 0.0625)
             nc.scalar.activation(
                 sg[t][:, :S],
@@ -216,7 +224,8 @@ def tile_picked_candesdedb_none_po_kernel(
                 bias=sbias[:, t : t + 1],
                 scale=sl_t[:, t : t + 1],
             )
-        other = [sb("other%d" % t, [P, S], F32, "s3" if t == 2 else None) for t in range(PACK)]
+        other = [sb("other%d" % t, [P, S], F32, "s0" if t == 2 else None) for t in range(PACK)]
+        first2 = sb("first2", [P, HALF], F32)
         out_rows = out_0.rearrange("(p t) c -> p t c", t=PACK)
 
         def finish(t, cols):
@@ -224,21 +233,30 @@ def tile_picked_candesdedb_none_po_kernel(
                 res[:, t, cols], diff[t][:, cols], -1.5 * 0.0625, s_ps[t][:, cols], ALU.mult, ALU.mult
             )
 
+        def on_vector(t, cols, copy_of_sg):
+            nc.vector.tensor_copy(copy_of_sg, sg[t][:, cols])
+            looked_up = sg[t][:].indirect(entries(n4_t, cols.start, cols.stop))
+            nc.vector.tensor_tensor(diff[t][:, cols], looked_up, copy_of_sg, ALU.subtract)
+            finish(t, cols)
+
+        def on_scalar(t, cols):
+            looked_up = sg[t][:].indirect(entries(n4_t, cols.start, cols.stop))
+            nc.scalar.activation(other[t][:, cols], looked_up, ACT.Copy)
+            nc.vector.tensor_tensor(diff[t][:, cols], other[t][:, cols], sg[t][:, cols], ALU.subtract)
+            finish(t, cols)
+
         for t in (0, 1):
-            nc.vector.tensor_copy(other[t][:], sg[t][:, :S])
-            nc.vector.tensor_tensor(diff[t][:], sg[t][:].indirect(n4_t[:]), other[t][:], ALU.subtract)
-            finish(t, slice(0, S))
+            on_vector(t, slice(0, S), other[t][:])
             nc.sync.dma_start(out_rows[:, t, :], res[:, t, :])
-        for t, pieces in ((2, ((0, S),)), (3, ((0, HALF), (HALF, S)))):
-            for lo, hi in pieces:
-                nc.scalar.activation(other[t][:, lo:hi], sg[t][:].indirect(entries(n4_t, lo, hi)), ACT.Copy)
-                nc.vector.tensor_tensor(diff[t][:, lo:hi], other[t][:, lo:hi], sg[t][:, lo:hi], ALU.subtract)
-                finish(t, slice(lo, hi))
+        on_vector(2, halves[0], first2[:])
+        on_scalar(3, halves[0])
+        for t in (2, 3):
+            on_scalar(t, halves[1])
             nc.sync.dma_start(out_rows[:, t, :], res[:, t, :])
 
-        rq, rs = quantise("res", res)
+        rq, rs = quantise("res", res, 384, halves)
         out_words = out_1[0].rearrange("p c r -> p (c r)").bitcast(I32)
-        for cols in reversed(halves):
+        for cols in halves:
             nc.sync.dma_start(out_words[:, cols], rq[:, cols].bitcast(I32))
         for q in range(4):
             queue = nc.scalar if q % 2 else nc.sync

@@ -196,7 +196,7 @@ def tile_picked_candesdedb_none_po_kernel(
         zq, zs = quantise("z", z, HALF, halves[::-1])
 
         for t in range(PACK):
-            for cols in reversed(halves):
+            for cols in halves[::-1] if t == 0 else (slice(0, S),):
                 nc.tensor.matmul_mx(
                     out=s_ps[t][:, cols],
                     lhsT=xc_w[:, P * t : P * (t + 1)].bitcast(FP8X4),
@@ -207,16 +207,12 @@ def tile_picked_candesdedb_none_po_kernel(
                     stop=True,
                 )
 
-        s = [sb("s%d" % t, [P, 2 * S], F32) for t in range(PACK - 1)]
+        s = [sb("s%d" % t, [P, 2 * S], F32) for t in range(PACK)]
         sg = [sb("sg%d" % t, [P, 2 * S], F32) for t in range(PACK)]
         diff = [sb("diff%d" % t, [P, S], F32) for t in range(PACK)]
         res = sb("res", [P, PACK, S], F32)
         for t in range(PACK):
-            if t < 3:
-                nc.vector.tensor_scalar(s[t][:, :S], s_ps[t][:], 0.0625, None, ALU.mult)
-            else:
-                s.append(sb("s3", [P, 2 * S], F32, "s0"))
-                nc.scalar.mul(s[t][:, :S], s_ps[t][:], 0.0625)
+            nc.vector.tensor_scalar(s[t][:, :S], s_ps[t][:], 0.0625, None, ALU.mult)
             nc.scalar.activation(
                 sg[t][:, :S],
                 s[t][:].indirect(n3_t[:]),
@@ -224,8 +220,7 @@ def tile_picked_candesdedb_none_po_kernel(
                 bias=sbias[:, t : t + 1],
                 scale=sl_t[:, t : t + 1],
             )
-        other = [sb("other%d" % t, [P, S], F32, "s0" if t == 2 else None) for t in range(PACK)]
-        first2 = sb("first2", [P, HALF], F32)
+        other = [sb("other%d" % t, [P, S], F32, "s3" if t == 2 else None) for t in range(PACK)]
         out_rows = out_0.rearrange("(p t) c -> p t c", t=PACK)
 
         def finish(t, cols):
@@ -233,28 +228,21 @@ def tile_picked_candesdedb_none_po_kernel(
                 res[:, t, cols], diff[t][:, cols], -1.5 * 0.0625, s_ps[t][:, cols], ALU.mult, ALU.mult
             )
 
-        def on_vector(t, cols, copy_of_sg):
-            nc.vector.tensor_copy(copy_of_sg, sg[t][:, cols])
-            looked_up = sg[t][:].indirect(entries(n4_t, cols.start, cols.stop))
-            nc.vector.tensor_tensor(diff[t][:, cols], looked_up, copy_of_sg, ALU.subtract)
-            finish(t, cols)
-
-        def on_scalar(t, cols):
-            looked_up = sg[t][:].indirect(entries(n4_t, cols.start, cols.stop))
-            nc.scalar.activation(other[t][:, cols], looked_up, ACT.Copy)
-            nc.vector.tensor_tensor(diff[t][:, cols], other[t][:, cols], sg[t][:, cols], ALU.subtract)
-            finish(t, cols)
-
         for t in (0, 1):
-            on_vector(t, slice(0, S), other[t][:])
+            nc.gpsimd.tensor_scalar(other[t][:], sg[t][:, :S], 1.0, 0.0, ALU.mult, ALU.add)
+            nc.vector.tensor_tensor(diff[t][:], sg[t][:].indirect(n4_t[:]), other[t][:], ALU.subtract)
+            finish(t, slice(0, S))
             nc.sync.dma_start(out_rows[:, t, :], res[:, t, :])
-        on_vector(2, halves[0], first2[:])
-        on_scalar(3, halves[0])
+        for cols in halves:
+            for t in (2, 3):
+                looked_up = sg[t][:].indirect(entries(n4_t, cols.start, cols.stop))
+                nc.scalar.activation(other[t][:, cols], looked_up, ACT.Copy)
+                nc.vector.tensor_tensor(diff[t][:, cols], other[t][:, cols], sg[t][:, cols], ALU.subtract)
+                finish(t, cols)
         for t in (2, 3):
-            on_scalar(t, halves[1])
             nc.sync.dma_start(out_rows[:, t, :], res[:, t, :])
 
-        rq, rs = quantise("res", res, 384, halves)
+        rq, rs = quantise("res", res, 320, halves)
         out_words = out_1[0].rearrange("p c r -> p (c r)").bitcast(I32)
         for cols in halves:
             nc.sync.dma_start(out_words[:, cols], rq[:, cols].bitcast(I32))

@@ -18,9 +18,16 @@ ACT = mybir.ActivationFunctionType
 
 P = 128
 PACK = 4
-LANE = 16
+QUADRANTS = 4
+PER_COLUMN = 16
+LINE = 4
 HALF = S // 2
-WIDE = 704
+FIRST, SECOND, ALL = slice(0, HALF), slice(HALF, S), slice(0, S)
+
+GATHER_WINDOW = 2 * S
+SCATTER_WINDOW = 704
+
+OUT_COLUMNS_ON_SCALAR = 320
 
 
 def tile_picked_candesdedb_none_po_kernel(
@@ -31,161 +38,155 @@ def tile_picked_candesdedb_none_po_kernel(
         pool = ctx.enter_context(tc.tile_pool(name="keep", bufs=1))
         psum = ctx.enter_context(tc.psum_pool(name="psum", bufs=1))
 
-        def sb(name, shape, dtype, after=None):
-            return pool.tile(shape, dtype, name=name, tag=after or name, align_bytes=64)
+        def sb(name, shape, dtype, reuse=None):
+            return pool.tile(shape, dtype, name=name, tag=reuse or name, align_bytes=64)
 
         def load_list(name, src):
-            tile = sb(name, [P, S // LANE], U16)
+            tile = sb(name, [P, S // PER_COLUMN], U16)
             nc.sync.dma_start(tile[:], src)
             return tile
 
-        def load_rows(name, src):
+        def load_row_values(name, src):
             tile = sb(name, [P, PACK], F32)
             nc.sync.dma_start(tile[:], src.rearrange("(p t) o -> p (t o)", t=PACK))
             return tile
 
-        def entries(lst, lo, hi):
-            return lst[:, lo // LANE : hi // LANE]
+        def entries(list_tile, cols):
+            return list_tile[:, cols.start // PER_COLUMN : cols.stop // PER_COLUMN]
 
-        xs = sb("xs", [P, T], U8)
-        ws_raw = sb("ws_raw", [P, H], U8)
-        nc.vector.memset(xs[:].bitcast(I32), 0)
-        nc.vector.memset(ws_raw[:].bitcast(I32), 0)
+        def live_rows(scale_tile, q):
+            return scale_tile[32 * q : 32 * q + 4, :].bitcast(I32)
+
+        def scale_rows(dram, q):
+            return dram[0, 4 * q : 4 * q + 4, :].bitcast(I32)
+
+        x_bytes = sb("x_bytes", [P, T], U8)
+        w_bytes_raw = sb("w_bytes_raw", [P, H], U8)
+        nc.vector.memset(x_bytes[:].bitcast(I32), 0)
+        nc.vector.memset(w_bytes_raw[:].bitcast(I32), 0)
 
         offs_t = load_list("offs_t", offs)
-        ww_raw = sb("ww_raw", [P, 2 * H], U8)
-        nc.scalar.dma_start(ww_raw[:].bitcast(I32), w1_words[0].bitcast(I32))
+        w_codes_raw = sb("w_codes_raw", [P, 2 * H], U8)
+        nc.scalar.dma_start(w_codes_raw[:].bitcast(I32), w1_words[0].bitcast(I32))
         cand_t = load_list("cand_t", cand)
-        for q in range(4):
-            queue = nc.sync if q < 2 else nc.scalar
-            queue.dma_start(xs[32 * q : 32 * q + 4, :].bitcast(I32), x_scales[0, 4 * q : 4 * q + 4, :].bitcast(I32))
-        xw = sb("xw", [P, T], I32)
-        nc.sync.dma_start(xw[:], x_words[0].rearrange("p n r -> p (n r)").bitcast(I32))
-        for q in range(4):
-            nc.sync.dma_start(
-                ws_raw[32 * q : 32 * q + 4, :].bitcast(I32), w1_scales[0, 4 * q : 4 * q + 4, :].bitcast(I32)
-            )
+        for q in range(QUADRANTS):
+            queue = nc.sync if q < QUADRANTS // 2 else nc.scalar
+            queue.dma_start(live_rows(x_bytes, q), scale_rows(x_scales, q))
+        x_codes = sb("x_codes", [P, T], I32)
+        nc.sync.dma_start(x_codes[:], x_words[0].rearrange("p n r -> p (n r)").bitcast(I32))
+        for q in range(QUADRANTS):
+            nc.sync.dma_start(live_rows(w_bytes_raw, q), scale_rows(w1_scales, q))
         n1_t = load_list("n1_t", n1)
-        tau_t = load_rows("tau_t", tau)
-        gs_t = load_rows("gs_t", gs)
-        sl_t = load_rows("sl_t", sl)
-        th_t = load_rows("th_t", th)
+        tau_t = load_row_values("tau_t", tau)
+        gs_t = load_row_values("gs_t", gs)
+        sl_t = load_row_values("sl_t", sl)
+        th_t = load_row_values("th_t", th)
         n2_t = load_list("n2_t", n2)
         n3_t = load_list("n3_t", n3)
         n4_t = load_list("n4_t", n4)
 
-        ww = sb("ww", [P, 2 * H], U8)
+        w_codes = sb("w_codes", [P, 2 * H], U8)
         nc.scalar.copy(
-            ww[:].bitcast(U16).rearrange("p (t m) -> p t m", t=PACK),
-            ww_raw[:].bitcast(U16).rearrange("p (m t) -> p t m", t=PACK),
+            w_codes[:].bitcast(U16).rearrange("p (t m) -> p t m", t=PACK),
+            w_codes_raw[:].bitcast(U16).rearrange("p (m t) -> p t m", t=PACK),
         )
 
-        xq_s = sb("xq_s", [P, S], U8)
-        xq_w = sb("xq_w", [P, S], U32)
-        nc.vector.tensor_copy(xq_s[:], xs[:].indirect(offs_t[:]))
-        ws = sb("ws", [P, H], U8)
+        picked_bytes = sb("picked_bytes", [P, S], U8)
+        picked_codes = sb("picked_codes", [P, S], U32)
+        nc.vector.tensor_copy(picked_bytes[:], x_bytes[:].indirect(offs_t[:]))
+        w_bytes = sb("w_bytes", [P, H], U8)
         nc.gpsimd.tensor_copy(
-            ws[:].rearrange("p (t m) -> p t m", t=PACK), ws_raw[:].rearrange("p (m t) -> p t m", t=PACK)
+            w_bytes[:].rearrange("p (t m) -> p t m", t=PACK), w_bytes_raw[:].rearrange("p (m t) -> p t m", t=PACK)
         )
-        nc.vector.tensor_copy(xq_w[:], xw[:].bitcast(U32).indirect(offs_t[:]))
+        nc.vector.tensor_copy(picked_codes[:], x_codes[:].bitcast(U32).indirect(offs_t[:]))
 
-        xc_s_raw = sb("xc_s_raw", [P, C], U8)
-        nc.vector.tensor_copy(xc_s_raw[:], xs[:].indirect(cand_t[:]))
+        cand_bytes_raw = sb("cand_bytes_raw", [P, C], U8)
+        nc.vector.tensor_copy(cand_bytes_raw[:], x_bytes[:].indirect(cand_t[:]))
+        cand_codes = sb("cand_codes", [P, C], U32, reuse="w_bytes_raw")
+        nc.vector.tensor_copy(
+            cand_codes[:].rearrange("p (t m) -> p m t", t=PACK), x_codes[:].bitcast(U32).indirect(cand_t[:])
+        )
 
-        xc_w = sb("xc_w", [P, C], U32, "ws_raw")
-        nc.vector.tensor_copy(xc_w[:].rearrange("p (t m) -> p m t", t=PACK), xw[:].bitcast(U32).indirect(cand_t[:]))
-
-        gs2 = sb("gs2", [P, PACK], F32)
-        ngs = sb("ngs", [P, PACK], F32)
-        nc.scalar.mul(gs2[:], gs_t[:], 2.0)
-        nc.scalar.mul(ngs[:], gs_t[:], -0.5)
-        nsl = sb("nsl", [P, PACK], F32)
-        sbias = sb("sbias", [P, PACK], F32)
-        nc.scalar.mul(nsl[:], sl_t[:], -1.0)
+        two_gs = sb("two_gs", [P, PACK], F32)
+        minus_half_gs = sb("minus_half_gs", [P, PACK], F32)
+        nc.scalar.mul(two_gs[:], gs_t[:], 2.0)
+        nc.scalar.mul(minus_half_gs[:], gs_t[:], -0.5)
+        minus_sl = sb("minus_sl", [P, PACK], F32)
+        sigmoid_bias = sb("sigmoid_bias", [P, PACK], F32)
+        nc.scalar.mul(minus_sl[:], sl_t[:], -1.0)
 
         y_ps = [psum.tile([P, S], F32, name="y_ps%d" % t) for t in range(PACK)]
         s_ps = [psum.tile([P, S], F32, name="s_ps%d" % t) for t in range(PACK)]
         for t in range(PACK):
             nc.tensor.matmul_mx(
                 out=y_ps[t][:],
-                lhsT=ww[:, 2 * P * t : 2 * P * (t + 1)].bitcast(FP4X4),
-                lhsT_scale=ws[:, P * t : P * (t + 1)],
-                rhs=xq_w[:].bitcast(FP8X4),
-                rhs_scale=xq_s[:],
+                lhsT=w_codes[:, 2 * P * t : 2 * P * (t + 1)].bitcast(FP4X4),
+                lhsT_scale=w_bytes[:, P * t : P * (t + 1)],
+                rhs=picked_codes[:].bitcast(FP8X4),
+                rhs_scale=picked_bytes[:],
                 start=True,
                 stop=True,
             )
 
-
-        y = [sb("y%d" % t, [P, 2 * S], F32) for t in range(PACK)]
+        y = [sb("y%d" % t, [P, GATHER_WINDOW], F32) for t in range(PACK)]
         top = [sb("top%d" % t, [P, 1], F32) for t in range(PACK)]
-        ebias = [sb("ebias%d" % t, [P, 1], F32) for t in range(PACK)]
+        exp_bias = [sb("exp_bias%d" % t, [P, 1], F32) for t in range(PACK)]
         ea = [sb("ea%d" % t, [P, S], F32) for t in range(PACK)]
-        pre = [sb("pre%d" % t, [P, S], F32) for t in range(PACK)]
-        for t in range(PACK):
-            nc.vector.tensor_scalar(y[t][:, :S], y_ps[t][:], 1.0, None, ALU.mult, ALU.max, accum_out=top[t][:])
-            nc.gpsimd.tensor_scalar(ebias[t][:], top[t][:], tau_t[:, t : t + 1], -1.0, ALU.mult, ALU.mult)
-            if t == 0:
-                nc.gpsimd.tensor_scalar(pre[t][:], y[t][:, :S], gs2[:, t : t + 1], 0.0, ALU.mult, ALU.add)
+        gy0_first = sb("gy0_first", [P, HALF], F32)
+
+        def exponentials(t):
             nc.scalar.activation(
-                ea[t][:], y[t][:].indirect(n1_t[:]), ACT.Exp, bias=ebias[t][:], scale=tau_t[:, t : t + 1]
+                ea[t][:], y[t][:].indirect(n1_t[:]), ACT.Exp, bias=exp_bias[t][:], scale=tau_t[:, t : t + 1]
             )
 
+        def copy_out_y(t):
+            nc.vector.tensor_scalar(y[t][:, ALL], y_ps[t][:], 1.0, None, ALU.mult, ALU.max, accum_out=top[t][:])
+            nc.gpsimd.tensor_scalar(exp_bias[t][:], top[t][:], tau_t[:, t : t + 1], -1.0, ALU.mult, ALU.mult)
 
-        nc.vector.tensor_scalar(pre[3][:], y[3][:, :S], gs2[:, 3:4], None, ALU.mult)
-        xc_s = sb("xc_s", [P, C], U8, "xq_s")
+        copy_out_y(0)
+        nc.gpsimd.tensor_scalar(gy0_first[:], y[0][:, FIRST], two_gs[:, 0:1], 0.0, ALU.mult, ALU.add)
+        exponentials(0)
+        for t in range(1, PACK):
+            copy_out_y(t)
+            exponentials(t)
+
+        gy3 = sb("gy3", [P, S], F32)
+        nc.vector.tensor_scalar(gy3[:], y[3][:, ALL], two_gs[:, 3:4], None, ALU.mult)
+        cand_bytes = sb("cand_bytes", [P, C], U8, reuse="picked_bytes")
         nc.vector.tensor_copy(
-            xc_s[:].rearrange("p (t m) -> p t m", t=PACK), xc_s_raw[:].rearrange("p (m t) -> p t m", t=PACK)
+            cand_bytes[:].rearrange("p (t m) -> p t m", t=PACK), cand_bytes_raw[:].rearrange("p (m t) -> p t m", t=PACK)
         )
-        nc.vector.tensor_tensor(sbias[:], nsl[:], th_t[:], ALU.mult)
-        z = sb("z", [P, PACK, S], BF16)
+        nc.vector.tensor_tensor(sigmoid_bias[:], minus_sl[:], th_t[:], ALU.mult)
 
-        def product(t):
-            nc.vector.scalar_tensor_tensor(pre[t][:], y_ps[t][:], gs2[:, t : t + 1], ea[t][:], ALU.mult, ALU.mult)
-
-        product(1)
-        ds2 = [sb("ds2_%d" % t, [P, WIDE if t == 3 else S], F32, "ea1" if t == 0 else None) for t in range(PACK)]
-
-        def scatter_half_on_vector(t, lo):
-            cols = slice(lo, lo + HALF)
-            nc.vector.tensor_tensor(
-                ds2[t][:].indirect(entries(n2_t, lo, lo + HALF)), pre[t][:, cols], ea[t][:, cols], ALU.mult
-            )
-
-        scatter_half_on_vector(0, 0)
-        product(2)
-        scatter_half_on_vector(0, HALF)
-        for lo in (0, HALF):
+        gds = [sb("gds%d" % t, [P, SCATTER_WINDOW if t == 3 else S], F32) for t in range(PACK)]
+        gsm = {t: sb("gsm%d" % t, [P, S], F32) for t in (1, 2)}
+        nc.vector.tensor_tensor(gds[0][:].indirect(entries(n2_t, FIRST)), gy0_first[:], ea[0][:, FIRST], ALU.mult)
+        for t in (1, 2):
+            nc.vector.scalar_tensor_tensor(gsm[t][:], y_ps[t][:], two_gs[:, t : t + 1], ea[t][:], ALU.mult, ALU.mult)
+        gy0_second = sb("gy0_second", [P, HALF], F32, reuse="ea1")
+        nc.gpsimd.tensor_scalar(gy0_second[:], y[0][:, SECOND], two_gs[:, 0:1], 0.0, ALU.mult, ALU.add)
+        nc.vector.tensor_tensor(gds[0][:].indirect(entries(n2_t, SECOND)), gy0_second[:], ea[0][:, SECOND], ALU.mult)
+        for cols in (FIRST, SECOND):
             for t in (1, 2):
-                nc.scalar.activation(
-                    ds2[t][:].indirect(entries(n2_t, lo, lo + HALF)), pre[t][:, lo : lo + HALF], ACT.Copy
-                )
-        nc.vector.tensor_tensor(ds2[3][:].indirect(n2_t[:]), pre[3][:], ea[3][:], ALU.mult)
-        halves = (slice(0, HALF), slice(HALF, S))
+                nc.scalar.activation(gds[t][:].indirect(entries(n2_t, cols)), gsm[t][:, cols], ACT.Copy)
+        nc.vector.tensor_tensor(gds[3][:].indirect(n2_t[:]), gy3[:], ea[3][:], ALU.mult)
 
-        def make_z(t, cols):
+        z = sb("z", [P, PACK, S], BF16)
+        for t, cols in ((0, ALL), (1, ALL), (3, ALL), (2, FIRST), (2, SECOND)):
             nc.vector.scalar_tensor_tensor(
-                z[:, t, cols], y_ps[t][:, cols], ngs[:, t : t + 1], ds2[t][:, cols], ALU.mult, ALU.add
+                z[:, t, cols], y_ps[t][:, cols], minus_half_gs[:, t : t + 1], gds[t][:, cols], ALU.mult, ALU.add
             )
 
-        for t in (0, 1, 3):
-            make_z(t, slice(0, S))
-        for cols in halves:
-            make_z(2, cols)
-
-        def quantise(name, src, scalar_columns, order):
+        def quantise(name, row_tiles, weaving, halves):
             woven = sb(name + "_woven", [P, S, PACK], BF16)
             codes = sb(name + "_codes", [P, S], U32)
             scales = sb(name + "_scales", [P, S], U8)
-            pieces = [(nc.scalar.copy, halves[0]), (nc.vector.tensor_copy, slice(scalar_columns, S))]
-            if scalar_columns > HALF:
-                pieces.append((nc.scalar.copy, slice(HALF, scalar_columns)))
-            for copy, cols in pieces:
+            for copy, cols in weaving:
                 copy(
-                    woven[:, cols, :].rearrange("p (c i) t -> p c t i", i=4),
-                    src[:, :, cols].rearrange("p t (c i) -> p c t i", i=4),
+                    woven[:, cols, :].rearrange("p (c i) t -> p c t i", i=LINE),
+                    row_tiles[:, :, cols].rearrange("p t (c i) -> p c t i", i=LINE),
                 )
-            for cols in order:
+            for cols in halves:
                 nc.vector.quantize_mx(
                     out=codes[:, cols].bitcast(FP8X4),
                     scales=scales[:, cols],
@@ -193,34 +194,35 @@ def tile_picked_candesdedb_none_po_kernel(
                 )
             return codes, scales
 
-        zq, zs = quantise("z", z, HALF, halves[::-1])
+        z_codes, z_scales = quantise(
+            "z", z, ((nc.scalar.copy, FIRST), (nc.vector.tensor_copy, SECOND)), (SECOND, FIRST)
+        )
 
-        for t in range(PACK):
-            for cols in halves[::-1] if t == 0 else (slice(0, S),):
-                nc.tensor.matmul_mx(
-                    out=s_ps[t][:, cols],
-                    lhsT=xc_w[:, P * t : P * (t + 1)].bitcast(FP8X4),
-                    lhsT_scale=xc_s[:, P * t : P * (t + 1)],
-                    rhs=zq[:, cols].bitcast(FP8X4),
-                    rhs_scale=zs[:, cols],
-                    start=True,
-                    stop=True,
-                )
+        for t, cols in ((0, SECOND), (0, FIRST), (1, ALL), (2, ALL), (3, ALL)):
+            nc.tensor.matmul_mx(
+                out=s_ps[t][:, cols],
+                lhsT=cand_codes[:, P * t : P * (t + 1)].bitcast(FP8X4),
+                lhsT_scale=cand_bytes[:, P * t : P * (t + 1)],
+                rhs=z_codes[:, cols].bitcast(FP8X4),
+                rhs_scale=z_scales[:, cols],
+                start=True,
+                stop=True,
+            )
 
-        s = [sb("s%d" % t, [P, 2 * S], F32) for t in range(PACK)]
-        sg = [sb("sg%d" % t, [P, 2 * S], F32) for t in range(PACK)]
+        s = [sb("s%d" % t, [P, GATHER_WINDOW], F32) for t in range(PACK)]
+        sg = [sb("sg%d" % t, [P, GATHER_WINDOW], F32) for t in range(PACK)]
         diff = [sb("diff%d" % t, [P, S], F32) for t in range(PACK)]
         res = sb("res", [P, PACK, S], F32)
         for t in range(PACK):
-            nc.vector.tensor_scalar(s[t][:, :S], s_ps[t][:], 0.0625, None, ALU.mult)
+            nc.vector.tensor_scalar(s[t][:, ALL], s_ps[t][:], 0.0625, None, ALU.mult)
             nc.scalar.activation(
-                sg[t][:, :S],
+                sg[t][:, ALL],
                 s[t][:].indirect(n3_t[:]),
                 ACT.Sigmoid,
-                bias=sbias[:, t : t + 1],
+                bias=sigmoid_bias[:, t : t + 1],
                 scale=sl_t[:, t : t + 1],
             )
-        other = [sb("other%d" % t, [P, S], F32, "s3" if t == 2 else None) for t in range(PACK)]
+
         out_rows = out_0.rearrange("(p t) c -> p t c", t=PACK)
 
         def finish(t, cols):
@@ -228,24 +230,34 @@ def tile_picked_candesdedb_none_po_kernel(
                 res[:, t, cols], diff[t][:, cols], -1.5 * 0.0625, s_ps[t][:, cols], ALU.mult, ALU.mult
             )
 
+        sg_copy = {t: sb("sg_copy%d" % t, [P, S], F32) for t in (0, 1)}
+        sg_n4 = {2: sb("sg_n4_2", [P, S], F32, reuse="s3"), 3: sb("sg_n4_3", [P, S], F32)}
         for t in (0, 1):
-            nc.gpsimd.tensor_scalar(other[t][:], sg[t][:, :S], 1.0, 0.0, ALU.mult, ALU.add)
-            nc.vector.tensor_tensor(diff[t][:], sg[t][:].indirect(n4_t[:]), other[t][:], ALU.subtract)
-            finish(t, slice(0, S))
+            nc.gpsimd.tensor_scalar(sg_copy[t][:], sg[t][:, ALL], 1.0, 0.0, ALU.mult, ALU.add)
+            nc.vector.tensor_tensor(diff[t][:], sg[t][:].indirect(n4_t[:]), sg_copy[t][:], ALU.subtract)
+            finish(t, ALL)
             nc.sync.dma_start(out_rows[:, t, :], res[:, t, :])
-        for cols in halves:
+        for cols in (FIRST, SECOND):
             for t in (2, 3):
-                looked_up = sg[t][:].indirect(entries(n4_t, cols.start, cols.stop))
-                nc.scalar.activation(other[t][:, cols], looked_up, ACT.Copy)
-                nc.vector.tensor_tensor(diff[t][:, cols], other[t][:, cols], sg[t][:, cols], ALU.subtract)
+                nc.scalar.activation(sg_n4[t][:, cols], sg[t][:].indirect(entries(n4_t, cols)), ACT.Copy)
+                nc.vector.tensor_tensor(diff[t][:, cols], sg_n4[t][:, cols], sg[t][:, cols], ALU.subtract)
                 finish(t, cols)
         for t in (2, 3):
             nc.sync.dma_start(out_rows[:, t, :], res[:, t, :])
 
-        rq, rs = quantise("res", res, 320, halves)
+        out_codes, out_scales = quantise(
+            "out",
+            res,
+            (
+                (nc.scalar.copy, FIRST),
+                (nc.vector.tensor_copy, slice(OUT_COLUMNS_ON_SCALAR, S)),
+                (nc.scalar.copy, slice(HALF, OUT_COLUMNS_ON_SCALAR)),
+            ),
+            (FIRST, SECOND),
+        )
         out_words = out_1[0].rearrange("p c r -> p (c r)").bitcast(I32)
-        for cols in halves:
-            nc.sync.dma_start(out_words[:, cols], rq[:, cols].bitcast(I32))
-        for q in range(4):
+        for cols in (FIRST, SECOND):
+            nc.sync.dma_start(out_words[:, cols], out_codes[:, cols].bitcast(I32))
+        for q in range(QUADRANTS):
             queue = nc.scalar if q % 2 else nc.sync
-            queue.dma_start(out_2[0, 4 * q : 4 * q + 4, :].bitcast(I32), rs[32 * q : 32 * q + 4, :].bitcast(I32))
+            queue.dma_start(scale_rows(out_2, q), live_rows(out_scales, q))

from contextlib import ExitStack

import concourse.mybir as mybir

K, T, S, H, C = 512, 2048, 512, 512, 512
FLOPS = 2 * K * H * S + 2 * K * C * S

F32 = mybir.dt.float32
BF16 = mybir.dt.bfloat16
I32 = mybir.dt.int32
U32 = mybir.dt.uint32
U16 = mybir.dt.uint16
U8 = mybir.dt.uint8
FP8X4 = mybir.dt.float8_e4m3fn_x4
FP4X4 = mybir.dt.float4_e2m1fn_x4
ALU = mybir.AluOpType
ACT = mybir.ActivationFunctionType

P = 128
PACK = 4
QUADRANTS = 4
PER_COLUMN = 16
LINE = 4
HALF = S // 2
FIRST, SECOND, ALL = slice(0, HALF), slice(HALF, S), slice(0, S)

GATHER_WINDOW = 2 * S
SCATTER_WINDOW = 704

OUT_COLUMNS_ON_SCALAR = 320


def tile_picked_candesdedb_none_po_kernel(
    tc, x_words, x_scales, w1_words, w1_scales, tau, gs, sl, th, offs, n1, n2, cand, n3, n4, out_0, out_1, out_2
):
    nc = tc.nc
    with ExitStack() as ctx:
        pool = ctx.enter_context(tc.tile_pool(name="keep", bufs=1))
        psum = ctx.enter_context(tc.psum_pool(name="psum", bufs=1))

        def sb(name, shape, dtype, reuse=None):
            return pool.tile(shape, dtype, name=name, tag=reuse or name, align_bytes=64)

        def load_list(name, src):
            tile = sb(name, [P, S // PER_COLUMN], U16)
            nc.sync.dma_start(tile[:], src)
            return tile

        def load_row_values(name, src):
            tile = sb(name, [P, PACK], F32)
            nc.sync.dma_start(tile[:], src.rearrange("(p t) o -> p (t o)", t=PACK))
            return tile

        def entries(list_tile, cols):
            return list_tile[:, cols.start // PER_COLUMN : cols.stop // PER_COLUMN]

        def live_rows(scale_tile, q):
            return scale_tile[32 * q : 32 * q + 4, :].bitcast(I32)

        def scale_rows(dram, q):
            return dram[0, 4 * q : 4 * q + 4, :].bitcast(I32)

        x_bytes = sb("x_bytes", [P, T], U8)
        w_bytes_raw = sb("w_bytes_raw", [P, H], U8)
        nc.vector.memset(x_bytes[:].bitcast(I32), 0)
        nc.vector.memset(w_bytes_raw[:].bitcast(I32), 0)

        offs_t = load_list("offs_t", offs)
        w_codes_raw = sb("w_codes_raw", [P, 2 * H], U8)
        nc.scalar.dma_start(w_codes_raw[:].bitcast(I32), w1_words[0].bitcast(I32))
        cand_t = load_list("cand_t", cand)
        for q in range(QUADRANTS):
            queue = nc.sync if q < QUADRANTS // 2 else nc.scalar
            queue.dma_start(live_rows(x_bytes, q), scale_rows(x_scales, q))
        x_codes = sb("x_codes", [P, T], I32)
        nc.sync.dma_start(x_codes[:], x_words[0].rearrange("p n r -> p (n r)").bitcast(I32))
        for q in range(QUADRANTS):
            nc.sync.dma_start(live_rows(w_bytes_raw, q), scale_rows(w1_scales, q))
        n1_t = load_list("n1_t", n1)
        tau_t = load_row_values("tau_t", tau)
        gs_t = load_row_values("gs_t", gs)
        sl_t = load_row_values("sl_t", sl)
        th_t = load_row_values("th_t", th)
        n2_t = load_list("n2_t", n2)
        n3_t = load_list("n3_t", n3)
        n4_t = load_list("n4_t", n4)

        w_codes = sb("w_codes", [P, 2 * H], U8)
        nc.scalar.copy(
            w_codes[:].bitcast(U16).rearrange("p (t m) -> p t m", t=PACK),
            w_codes_raw[:].bitcast(U16).rearrange("p (m t) -> p t m", t=PACK),
        )

        picked_bytes = sb("picked_bytes", [P, S], U8)
        picked_codes = sb("picked_codes", [P, S], U32)
        nc.vector.tensor_copy(picked_bytes[:], x_bytes[:].indirect(offs_t[:]))
        w_bytes = sb("w_bytes", [P, H], U8)
        nc.gpsimd.tensor_copy(
            w_bytes[:].rearrange("p (t m) -> p t m", t=PACK), w_bytes_raw[:].rearrange("p (m t) -> p t m", t=PACK)
        )
        nc.vector.tensor_copy(picked_codes[:], x_codes[:].bitcast(U32).indirect(offs_t[:]))

        cand_bytes_raw = sb("cand_bytes_raw", [P, C], U8)
        nc.vector.tensor_copy(cand_bytes_raw[:], x_bytes[:].indirect(cand_t[:]))
        cand_codes = sb("cand_codes", [P, C], U32, reuse="w_bytes_raw")
        nc.vector.tensor_copy(
            cand_codes[:].rearrange("p (t m) -> p m t", t=PACK), x_codes[:].bitcast(U32).indirect(cand_t[:])
        )

        two_gs = sb("two_gs", [P, PACK], F32)
        minus_half_gs = sb("minus_half_gs", [P, PACK], F32)
        nc.scalar.mul(two_gs[:], gs_t[:], 2.0)
        nc.scalar.mul(minus_half_gs[:], gs_t[:], -0.5)
        minus_sl = sb("minus_sl", [P, PACK], F32)
        sigmoid_bias = sb("sigmoid_bias", [P, PACK], F32)
        nc.scalar.mul(minus_sl[:], sl_t[:], -1.0)

        y_ps = [psum.tile([P, S], F32, name="y_ps%d" % t) for t in range(PACK)]
        s_ps = [psum.tile([P, S], F32, name="s_ps%d" % t) for t in range(PACK)]
        for t in range(PACK):
            nc.tensor.matmul_mx(
                out=y_ps[t][:],
                lhsT=w_codes[:, 2 * P * t : 2 * P * (t + 1)].bitcast(FP4X4),
                lhsT_scale=w_bytes[:, P * t : P * (t + 1)],
                rhs=picked_codes[:].bitcast(FP8X4),
                rhs_scale=picked_bytes[:],
                start=True,
                stop=True,
            )

        y = [sb("y%d" % t, [P, GATHER_WINDOW], F32) for t in range(PACK)]
        top = [sb("top%d" % t, [P, 1], F32) for t in range(PACK)]
        exp_bias = [sb("exp_bias%d" % t, [P, 1], F32) for t in range(PACK)]
        ea = [sb("ea%d" % t, [P, S], F32) for t in range(PACK)]
        gy0_first = sb("gy0_first", [P, HALF], F32)

        def exponentials(t):
            nc.scalar.activation(
                ea[t][:], y[t][:].indirect(n1_t[:]), ACT.Exp, bias=exp_bias[t][:], scale=tau_t[:, t : t + 1]
            )

        def copy_out_y(t):
            nc.vector.tensor_scalar(y[t][:, ALL], y_ps[t][:], 1.0, None, ALU.mult, ALU.max, accum_out=top[t][:])
            nc.gpsimd.tensor_scalar(exp_bias[t][:], top[t][:], tau_t[:, t : t + 1], -1.0, ALU.mult, ALU.mult)

        copy_out_y(0)
        nc.gpsimd.tensor_scalar(gy0_first[:], y[0][:, FIRST], two_gs[:, 0:1], 0.0, ALU.mult, ALU.add)
        exponentials(0)
        for t in range(1, PACK):
            copy_out_y(t)
            exponentials(t)

        gy3 = sb("gy3", [P, S], F32)
        nc.vector.tensor_scalar(gy3[:], y[3][:, ALL], two_gs[:, 3:4], None, ALU.mult)
        cand_bytes = sb("cand_bytes", [P, C], U8, reuse="picked_bytes")
        nc.vector.tensor_copy(
            cand_bytes[:].rearrange("p (t m) -> p t m", t=PACK), cand_bytes_raw[:].rearrange("p (m t) -> p t m", t=PACK)
        )
        nc.vector.tensor_tensor(sigmoid_bias[:], minus_sl[:], th_t[:], ALU.mult)

        gds = [sb("gds%d" % t, [P, SCATTER_WINDOW if t == 3 else S], F32) for t in range(PACK)]
        gsm = {t: sb("gsm%d" % t, [P, S], F32) for t in (1, 2)}
        nc.vector.tensor_tensor(gds[0][:].indirect(entries(n2_t, FIRST)), gy0_first[:], ea[0][:, FIRST], ALU.mult)
        for t in (1, 2):
            nc.vector.scalar_tensor_tensor(gsm[t][:], y_ps[t][:], two_gs[:, t : t + 1], ea[t][:], ALU.mult, ALU.mult)
        gy0_second = sb("gy0_second", [P, HALF], F32, reuse="ea1")
        nc.gpsimd.tensor_scalar(gy0_second[:], y[0][:, SECOND], two_gs[:, 0:1], 0.0, ALU.mult, ALU.add)
        nc.vector.tensor_tensor(gds[0][:].indirect(entries(n2_t, SECOND)), gy0_second[:], ea[0][:, SECOND], ALU.mult)
        for cols in (FIRST, SECOND):
            for t in (1, 2):
                nc.scalar.activation(gds[t][:].indirect(entries(n2_t, cols)), gsm[t][:, cols], ACT.Copy)
        nc.vector.tensor_tensor(gds[3][:].indirect(n2_t[:]), gy3[:], ea[3][:], ALU.mult)

        z = sb("z", [P, PACK, S], BF16)
        for t, cols in ((0, ALL), (1, ALL), (3, ALL), (2, FIRST), (2, SECOND)):
            nc.vector.scalar_tensor_tensor(
                z[:, t, cols], y_ps[t][:, cols], minus_half_gs[:, t : t + 1], gds[t][:, cols], ALU.mult, ALU.add
            )

        def quantise(name, row_tiles, weaving, halves):
            woven = sb(name + "_woven", [P, S, PACK], BF16)
            codes = sb(name + "_codes", [P, S], U32)
            scales = sb(name + "_scales", [P, S], U8)
            for copy, cols in weaving:
                copy(
                    woven[:, cols, :].rearrange("p (c i) t -> p c t i", i=LINE),
                    row_tiles[:, :, cols].rearrange("p t (c i) -> p c t i", i=LINE),
                )
            for cols in halves:
                nc.vector.quantize_mx(
                    out=codes[:, cols].bitcast(FP8X4),
                    scales=scales[:, cols],
                    in_=woven[:, cols, :].rearrange("p c t -> p (c t)"),
                )
            return codes, scales

        z_codes, z_scales = quantise(
            "z", z, ((nc.scalar.copy, FIRST), (nc.vector.tensor_copy, SECOND)), (SECOND, FIRST)
        )

        for t, cols in ((0, SECOND), (0, FIRST), (1, ALL), (2, ALL), (3, ALL)):
            nc.tensor.matmul_mx(
                out=s_ps[t][:, cols],
                lhsT=cand_codes[:, P * t : P * (t + 1)].bitcast(FP8X4),
                lhsT_scale=cand_bytes[:, P * t : P * (t + 1)],
                rhs=z_codes[:, cols].bitcast(FP8X4),
                rhs_scale=z_scales[:, cols],
                start=True,
                stop=True,
            )

        s = [sb("s%d" % t, [P, GATHER_WINDOW], F32) for t in range(PACK)]
        sg = [sb("sg%d" % t, [P, GATHER_WINDOW], F32) for t in range(PACK)]
        diff = [sb("diff%d" % t, [P, S], F32) for t in range(PACK)]
        res = sb("res", [P, PACK, S], F32)
        for t in range(PACK):
            nc.vector.tensor_scalar(s[t][:, ALL], s_ps[t][:], 0.0625, None, ALU.mult)
            nc.scalar.activation(
                sg[t][:, ALL],
                s[t][:].indirect(n3_t[:]),
                ACT.Sigmoid,
                bias=sigmoid_bias[:, t : t + 1],
                scale=sl_t[:, t : t + 1],
            )

        out_rows = out_0.rearrange("(p t) c -> p t c", t=PACK)

        def finish(t, cols):
            nc.vector.scalar_tensor_tensor(
                res[:, t, cols], diff[t][:, cols], -1.5 * 0.0625, s_ps[t][:, cols], ALU.mult, ALU.mult
            )

        sg_copy = {t: sb("sg_copy%d" % t, [P, S], F32) for t in (0, 1)}
        sg_n4 = {2: sb("sg_n4_2", [P, S], F32, reuse="s3"), 3: sb("sg_n4_3", [P, S], F32)}
        for t in (0, 1):
            nc.gpsimd.tensor_scalar(sg_copy[t][:], sg[t][:, ALL], 1.0, 0.0, ALU.mult, ALU.add)
            nc.vector.tensor_tensor(diff[t][:], sg[t][:].indirect(n4_t[:]), sg_copy[t][:], ALU.subtract)
            finish(t, ALL)
            nc.sync.dma_start(out_rows[:, t, :], res[:, t, :])
        for cols in (FIRST, SECOND):
            for t in (2, 3):
                nc.scalar.activation(sg_n4[t][:, cols], sg[t][:].indirect(entries(n4_t, cols)), ACT.Copy)
                nc.vector.tensor_tensor(diff[t][:, cols], sg_n4[t][:, cols], sg[t][:, cols], ALU.subtract)
                finish(t, cols)
        for t in (2, 3):
            nc.sync.dma_start(out_rows[:, t, :], res[:, t, :])

        out_codes, out_scales = quantise(
            "out",
            res,
            (
                (nc.scalar.copy, FIRST),
                (nc.vector.tensor_copy, slice(OUT_COLUMNS_ON_SCALAR, S)),
                (nc.scalar.copy, slice(HALF, OUT_COLUMNS_ON_SCALAR)),
            ),
            (FIRST, SECOND),
        )
        out_words = out_1[0].rearrange("p c r -> p (c r)").bitcast(I32)
        for cols in (FIRST, SECOND):
            nc.sync.dma_start(out_words[:, cols], out_codes[:, cols].bitcast(I32))
        for q in range(QUADRANTS):
            queue = nc.scalar if q % 2 else nc.sync
            queue.dma_start(scale_rows(out_2, q), live_rows(out_scales, q))
